import numpy as np
import ml_dtypes


def mxq(x, axis, fmt="e4m3"):
    dtype, down = {"e4m3": (ml_dtypes.float8_e4m3fn, 7), "e5m2": (ml_dtypes.float8_e5m2, 14)}[fmt]
    v = np.moveaxis(np.asarray(x, np.float32).astype(ml_dtypes.bfloat16).astype(np.float64), axis, -1)
    blocks = v.reshape(v.shape[:-1] + (-1, 32))
    amax = np.abs(blocks).max(-1, keepdims=True)
    byte = np.maximum(np.where(amax > 0, np.frexp(amax)[1] - 1 + 127, 0) - down, 1)
    scale = np.exp2(byte - 127.0)
    codes = (blocks / scale).astype(np.float32).astype(dtype).astype(np.float64)
    return np.moveaxis((codes * scale).reshape(v.shape), -1, axis)


WIDE = False


def mx_kscale(k):
    if not WIDE:
        return np.ones(k)
    levels = np.array([10, -10, 5, -5, 0])
    if k % 512:
        return np.exp2(np.random.permutation(np.resize(levels, k // 32))).repeat(32)
    a = np.empty((k // 512, 16))
    for p in range(k // 512):
        a[p, :8] = np.random.permutation(np.resize(levels, 8))
        for g in range(8):
            far = levels[np.abs(levels - a[p, g]) >= 10]
            a[p, g + 8] = far[np.random.randint(len(far))]
    return np.exp2(a.ravel()).repeat(32)


def f64(x):
    return np.asarray(x).astype(np.float64)


def striped(idx):
    return np.tile(idx.reshape(-1, 16).T, (8, 1)).astype(np.uint16)


def unstriped(offs):
    return offs[:16].T.reshape(-1).astype(np.int64)


E2M1 = np.array([0.0, 0.5, 1.0, 1.5, 2.0, 3.0, 4.0, 6.0, -0.0, -0.5, -1.0, -1.5, -2.0, -3.0, -4.0, -6.0])


def pack_weight(w, fmt):
    k, n = w.shape
    w = f64(np.asarray(w, np.float32).astype(ml_dtypes.bfloat16)).reshape(k // 32, 32, n)
    amax = np.abs(w).max(1)
    if fmt == "e4m3":
        byte = np.frexp(amax)[1] - 1 + 127 - 7
    else:
        mant, ex = np.frexp(amax / 6.0)
        byte = np.where(mant > 0.5, ex, ex - 1) + 127
    byte = np.clip(np.where(amax > 0, byte, 1), 1, 254)
    scaled = (w * np.exp2(127.0 - byte)[:, None, :]).reshape(k, n).astype(np.float32)
    by_word = np.ascontiguousarray(scaled.reshape(k // 512, 128, 4, n).transpose(0, 1, 3, 2))
    if fmt == "e4m3":
        words = by_word.astype(ml_dtypes.float8_e4m3fn).view(np.uint8)
    else:
        c = by_word.astype(ml_dtypes.float4_e2m1fn).view(np.uint8) & 0xF
        words = (c[..., 0::2] | (c[..., 1::2] << 4)).reshape(k // 512, 128, 2 * n)
    return np.ascontiguousarray(words), np.ascontiguousarray(byte.astype(np.uint8).reshape(k // 512, 16, n))


def unpack_weight(words, scales, fmt):
    g, _, n = scales.shape
    words = np.ascontiguousarray(words).reshape(g, 128, n, -1)
    if fmt == "e4m3":
        vals = words.view(ml_dtypes.float8_e4m3fn).astype(np.float64)
    else:
        nib = np.empty((g, 128, n, 4), np.uint8)
        nib[..., 0::2] = words & 0xF
        nib[..., 1::2] = words >> 4
        vals = E2M1[nib]
    vals = vals * np.repeat(np.exp2(scales.astype(np.float64) - 127.0), 8, axis=1)[..., None]
    return vals.transpose(0, 1, 3, 2).reshape(g * 512, n)


K, T, E, C, N = 1536, 1024, 16, 256, 128
TOP = 4


def by_expert(wq, xq):
    return np.concatenate([wq[e].T @ xq[:, e * C:(e + 1) * C] for e in range(E)], axis=1)


def setup_inputs():
    n = np.random.standard_normal
    s = mx_kscale(K)[:, None]
    deal = np.repeat(np.arange(E), C).reshape(TOP, T)[:, np.random.permutation(T)]
    deal = np.take_along_axis(deal, np.argsort(np.random.rand(TOP, T), axis=0), axis=0)
    for _ in range(8):
        s_, t_ = np.random.permutation(T).reshape(2, -1); r = np.random.randint(TOP, size=T // 2); x, y = deal[r, s_].copy(), deal[r, t_].copy()
        ok = ~((deal[:, s_] == y).any(0) | (deal[:, t_] == x).any(0)); deal[r[ok], s_[ok]] = y[ok]; deal[r[ok], t_[ok]] = x[ok]
    order = np.lexsort((np.random.rand(TOP * T), deal.reshape(-1)))
    slot_token = order % T; pos = np.empty(TOP * T, np.int64); pos[order] = np.arange(TOP * T); pos = pos.reshape(TOP, T)
    g = np.random.uniform(0.5, 1.5, (TOP, T)); g = g / g.sum(0)
    w = [pack_weight(m, "e2m1") for m in n((E, K, N)) / np.sqrt(K) / s[None]]
    return {
        "xT": (n((K, T)) * s).astype(np.float32),
        "w_words": np.stack([m[0] for m in w]),
        "w_scales": np.stack([m[1] for m in w]),
        "b": (0.3 * n((N, E))).astype(np.float32),
        "gate": np.stack([np.tile(r, (N, 1)) for r in g]).astype(np.float32),
        "offs": striped(slot_token),
        "pos1": striped(pos[0]),
        "pos2": striped(pos[1]),
        "pos3": striped(pos[2]),
        "pos4": striped(pos[3]),
    }


def reference(xT, w_words, w_scales, b, gate, offs, pos1, pos2, pos3, pos4):
    idx = unstriped(offs)
    w = np.stack([unpack_weight(w_words[e], w_scales[e], "e2m1") for e in range(E)])
    xq = mxq(f64(xT)[:, idx], 0, "e4m3")
    y = by_expert(w, xq)
    y = y + np.repeat(f64(b), C, axis=1)
    return sum(f64(gate[r]) * y[:, unstriped(p)] for r, p in enumerate((pos1, pos2, pos3, pos4)))

@@ -1,0 +1,189 @@
+from contextlib import ExitStack
+
+import concourse.mybir as mybir
+
+K, T, E, C, N, TOP = 1536, 1024, 16, 256, 128, 4
+SLOTS = E * C
+P = 128
+PASSES = 3
+K_PASS = 512
+FLOPS = 2 * SLOTS * K * N
+
+F32 = mybir.dt.float32
+BF16 = mybir.dt.bfloat16
+U32 = mybir.dt.uint32
+I32 = mybir.dt.int32
+U16 = mybir.dt.uint16
+U8 = mybir.dt.uint8
+FP8X4 = mybir.dt.float8_e4m3fn_x4
+FP4X4 = mybir.dt.float4_e2m1fn_x4
+MULT = mybir.AluOpType.mult
+ADD = mybir.AluOpType.add
+IDENTITY = mybir.ActivationFunctionType.Identity
+
+
+def tile_moe_tk_lin_bias_kernel(
+    tc, xT, w_words, w_scales, b, gate, offs, pos1, pos2, pos3, pos4, out
+):
+    nc = tc.nc
+    with ExitStack() as ctx:
+        keep = ctx.enter_context(tc.tile_pool(name="keep", bufs=1))
+        psum = ctx.enter_context(tc.psum_pool(name="psum", bufs=8))
+
+        offs_sb = keep.tile([P, SLOTS // 16], U16, name="offs_sb")
+        pos_sb = [keep.tile([P, T // 16], U16, name=f"pos_sb{r}") for r in range(TOP)]
+
+        chunks = [[256, 256, 256, 256], [512, 512], [512, 512]]
+        raw, rows = {}, {}
+        for a in range(PASSES):
+            t0 = 0
+            for c, width in enumerate(chunks[a]):
+                raw[a, c] = keep.tile([P, 4, width], F32, name=f"raw{a}_{c}")
+                rows[a, c] = keep.tile([P, width, 4], BF16, name=f"rows{a}_{c}", align_bytes=64)
+                t0 += width
+        words = [keep.tile([P, T], U32, name=f"words{a}", align_bytes=64) for a in range(PASSES)]
+        bytes_all = keep.tile([P, T], U8, name="bytes_all", align_bytes=64)
+        slot_words = [keep.tile([P, SLOTS], U32, name=f"slot_words{a}", align_bytes=64) for a in range(PASSES)]
+        slot_bytes = keep.tile([P, SLOTS], U8, name="slot_bytes", align_bytes=64)
+        shifted = [keep.tile([P, SLOTS], U8, name=f"shifted{a}", align_bytes=64) for a in (1, 2)]
+        planes = [slot_bytes, shifted[0], shifted[1]]
+        w_sb = keep.tile([P, E * PASSES, 2 * N], U8, name="w_sb", align_bytes=64)
+        ws_sb = keep.tile([P, E * PASSES, N], U8, name="ws_sb", align_bytes=64)
+        b_sb = keep.tile([P, E], F32, name="b_sb")
+        gate_sb = keep.tile([P, TOP, T], F32, name="gate_sb")
+        y = keep.tile([P, SLOTS], F32, name="y")
+
+        nc.vector.memset(bytes_all[:].bitcast(I32), 0)
+        nc.vector.memset(ws_sb[:].rearrange("p a n -> p (a n)").bitcast(I32), 0)
+        for s in shifted:
+            nc.vector.memset(s[:].bitcast(I32), 0)
+
+        def load_x(a, c):
+            t0 = sum(chunks[a][:c])
+            width = chunks[a][c]
+            view = xT[a * K_PASS : (a + 1) * K_PASS, t0 : t0 + width]
+            nc.sync.dma_start(out=raw[a, c][:], in_=view.rearrange("(p j) t -> p j t", j=4))
+
+        for c in range(3):
+            load_x(0, c)
+        nc.sync.dma_start(offs_sb[:], offs)
+        load_x(0, 3)
+        for a in (1, 2):
+            for c in range(2):
+                load_x(a, c)
+        ws_rows = w_scales.rearrange("e a q n -> q (e a) n")
+        for q in range(4):
+            nc.sync.dma_start(
+                out=ws_sb[32 * q : 32 * q + 4, :, :].bitcast(I32), in_=ws_rows[4 * q : 4 * q + 4].bitcast(I32)
+            )
+        w_rows = w_words.rearrange("e a p c -> p (e a) c")
+        for g in range(4):
+            sl = slice(12 * g, 12 * g + 12)
+            nc.sync.dma_start(out=w_sb[:, sl, :].bitcast(I32), in_=w_rows[:, sl, :].bitcast(I32))
+        nc.sync.dma_start(b_sb[:], b)
+        for r, p in enumerate((pos1, pos2, pos3, pos4)):
+            nc.sync.dma_start(pos_sb[r][:], p)
+        gate_rows = gate.rearrange("r p t -> p r t")
+        for r in range(TOP):
+            nc.sync.dma_start(out=gate_sb[:, r, :], in_=gate_rows[:, r, :])
+
+        def cast(a, c, engine):
+            src = raw[a, c][:].rearrange("p j t -> p t j")
+            if engine == "v":
+                nc.vector.tensor_copy(out=rows[a, c][:], in_=src)
+            else:
+                nc.scalar.copy(out=rows[a, c][:], in_=src)
+
+        def quant(a, c):
+            t0 = sum(chunks[a][:c])
+            width = chunks[a][c]
+            nc.vector.quantize_mx(
+                out=words[a][:, t0 : t0 + width].bitcast(FP8X4),
+                scales=bytes_all[4 * a : P, t0 : t0 + width],
+                in_=rows[a, c][:].rearrange("p t j -> p (t j)"),
+            )
+
+        groups = [(0, 3), (3, 6), (6, 9), (9, 12), (12, 15), (15, 16)]
+
+        def offsets(e0, e1):
+            return offs_sb[:, e0 * C // 16 : e1 * C // 16]
+
+        def gather_words(a, e0, e1):
+            nc.vector.tensor_copy(
+                out=slot_words[a][:, e0 * C : e1 * C], in_=words[a][:].indirect(offsets(e0, e1))
+            )
+
+        cast(0, 0, "v")
+        for c in range(1, 4):
+            cast(0, c, "v")
+            quant(0, c - 1)
+        quant(0, 3)
+        for a in (1, 2):
+            for c in range(2):
+                cast(a, c, "s")
+        for e0, e1 in groups:
+            gather_words(0, e0, e1)
+        for a in (1, 2):
+            for c in range(2):
+                quant(a, c)
+        for e0, e1 in groups:
+            cols = slice(e0 * C, e1 * C)
+            nc.vector.tensor_copy(out=slot_bytes[:, cols], in_=bytes_all[:].indirect(offsets(e0, e1)))
+            for a in (1, 2):
+                nc.sync.dma_start(
+                    out=shifted[a - 1][0 : P - 4 * a, cols].bitcast(I32),
+                    in_=slot_bytes[4 * a : P, cols].bitcast(I32),
+                )
+        for e0, e1 in groups:
+            gather_words(1, e0, e1)
+            gather_words(2, e0, e1)
+            for e in range(e0, e1):
+                bank = psum.tile([N, 512], F32, name="bank")
+                for h in range(2):
+                    cols = slice(e * C + h * 128, e * C + h * 128 + 128)
+                    for a in range(PASSES):
+                        nc.tensor.matmul_mx(
+                            out=bank[:, h * 128 : h * 128 + 128],
+                            lhsT=w_sb[:, e * PASSES + a, :].bitcast(FP4X4),
+                            lhsT_scale=ws_sb[:, e * PASSES + a, :],
+                            rhs=slot_words[a][:, cols].bitcast(FP8X4),
+                            rhs_scale=planes[a][:, cols],
+                            start=(a == 0),
+                            stop=(a == PASSES - 1),
+                        )
+                nc.scalar.activation(
+                    out=y[:, e * C : (e + 1) * C], in_=bank[:, 0:C], func=IDENTITY, bias=b_sb[:, e : e + 1]
+                )
+
+        halves = [(0, 512), (512, 1024)]
+        prod = {}
+        for i, (t0, t1) in enumerate(halves):
+            for r in range(TOP):
+                prod[i, r] = keep.tile([P, t1 - t0], F32, name=f"prod{i}_{r}")
+        sums = {}
+        for i, (t0, t1) in enumerate(halves):
+            for s in range(3):
+                sums[i, s] = keep.tile([P, t1 - t0], F32, name=f"sums{i}_{s}")
+
+        def pick(i, r):
+            t0, t1 = halves[i]
+            nc.vector.tensor_tensor(
+                prod[i, r][:], y[:].indirect(pos_sb[r][:, t0 // 16 : t1 // 16]), gate_sb[:, r, t0:t1], MULT
+            )
+
+        def add(i, s):
+            pairs = [(prod[i, 0], prod[i, 1]), (prod[i, 2], prod[i, 3]), (sums[i, 0], sums[i, 1])]
+            nc.vector.tensor_tensor(sums[i, s][:], pairs[s][0][:], pairs[s][1][:], ADD)
+
+        for r in range(TOP):
+            pick(0, r)
+        for r in range(TOP):
+            pick(1, r)
+            if r < 3:
+                add(0, r)
+        t0, t1 = halves[0]
+        nc.sync.dma_start(out=out[:, t0:t1], in_=sums[0, 2][:])
+        for s in range(3):
+            add(1, s)
+        t0, t1 = halves[1]
+        nc.sync.dma_start(out=out[:, t0:t1], in_=sums[1, 2][:])

@@ -1,6 +1,7 @@
 from contextlib import ExitStack
 
 import concourse.mybir as mybir
+from concourse.masks import make_identity
 
 K, T, E, C, N, TOP = 1536, 1024, 16, 256, 128, 4
 SLOTS = E * C
@@ -28,21 +29,14 @@ def tile_moe_tk_lin_bias_kernel(
     nc = tc.nc
     with ExitStack() as ctx:
         keep = ctx.enter_context(tc.tile_pool(name="keep", bufs=1))
+        stage = ctx.enter_context(tc.tile_pool(name="stage", bufs=4))
         psum = ctx.enter_context(tc.psum_pool(name="psum", bufs=8))
 
         offs_sb = keep.tile([P, SLOTS // 16], U16, name="offs_sb")
         pos_sb = [keep.tile([P, T // 16], U16, name=f"pos_sb{r}") for r in range(TOP)]
-
-        chunks = [[256, 256, 256, 256], [512, 512], [512, 512]]
-        raw, rows = {}, {}
-        for a in range(PASSES):
-            t0 = 0
-            for c, width in enumerate(chunks[a]):
-                raw[a, c] = keep.tile([P, 4, width], F32, name=f"raw{a}_{c}")
-                rows[a, c] = keep.tile([P, width, 4], BF16, name=f"rows{a}_{c}", align_bytes=64)
-                t0 += width
-        words = [keep.tile([P, T], U32, name=f"words{a}", align_bytes=64) for a in range(PASSES)]
-        bytes_all = keep.tile([P, T], U8, name="bytes_all", align_bytes=64)
+        windows = (2 * T, 2 * T, T)
+        words = [keep.tile([P, windows[a]], U32, name=f"words{a}", align_bytes=64) for a in range(PASSES)]
+        bytes_all = keep.tile([P, 2 * T], U8, name="bytes_all", align_bytes=64)
         slot_words = [keep.tile([P, SLOTS], U32, name=f"slot_words{a}", align_bytes=64) for a in range(PASSES)]
         slot_bytes = keep.tile([P, SLOTS], U8, name="slot_bytes", align_bytes=64)
         shifted = [keep.tile([P, SLOTS], U8, name=f"shifted{a}", align_bytes=64) for a in (1, 2)]
@@ -52,25 +46,77 @@ def tile_moe_tk_lin_bias_kernel(
         b_sb = keep.tile([P, E], F32, name="b_sb")
         gate_sb = keep.tile([P, TOP, T], F32, name="gate_sb")
         y = keep.tile([P, SLOTS], F32, name="y")
+        ident = keep.tile([P, P], F32, name="ident")
 
-        nc.vector.memset(bytes_all[:].bitcast(I32), 0)
+        nc.vector.memset(words[0][:, T : 2 * T].bitcast(I32), 0)
+        nc.gpsimd.memset(bytes_all[:].bitcast(I32), 0)
         nc.vector.memset(ws_sb[:].rearrange("p a n -> p (a n)").bitcast(I32), 0)
+        nc.vector.memset(words[1][:, T : 2 * T].bitcast(I32), 0)
         for s in shifted:
-            nc.vector.memset(s[:].bitcast(I32), 0)
+            nc.gpsimd.memset(s[:].bitcast(I32), 0)
+        make_identity(nc, ident[:])
+
+        chunks = [[512, 256, 256], [512, 512], [512, 512]]
+        parts = [
+            [(0, 256, "v"), (256, 512, "s"), (512, 768, "v"), (768, 896, "v"), (896, 1024, "s")],
+            [(0, 512, "s"), (512, 1024, "s")],
+            [(0, 512, "s"), (512, 1024, "s")],
+        ]
+        raw, rows = {}, {}
 
         def load_x(a, c):
             t0 = sum(chunks[a][:c])
             width = chunks[a][c]
+            raw[a, c] = stage.tile([P, 4, width], F32, name=f"raw{width}")
             view = xT[a * K_PASS : (a + 1) * K_PASS, t0 : t0 + width]
             nc.sync.dma_start(out=raw[a, c][:], in_=view.rearrange("(p j) t -> p j t", j=4))
 
-        for c in range(3):
+        for c in range(len(chunks[0])):
             load_x(0, c)
         nc.sync.dma_start(offs_sb[:], offs)
-        load_x(0, 3)
-        for a in (1, 2):
-            for c in range(2):
-                load_x(a, c)
+        for c in range(len(chunks[1])):
+            load_x(1, c)
+
+        def cast(a, t0, t1, engine):
+            rows[a, t0] = keep.tile([P, t1 - t0, 4], BF16, name=f"rows{a}_{t0}", align_bytes=64)
+            start = 0
+            for c, width in enumerate(chunks[a]):
+                if start <= t0 < start + width:
+                    src = raw[a, c][:, :, t0 - start : t1 - start].rearrange("p j t -> p t j")
+                start += width
+            if engine == "v":
+                nc.vector.tensor_copy(out=rows[a, t0][:], in_=src)
+            else:
+                nc.scalar.copy(out=rows[a, t0][:], in_=src)
+
+        def quant(a, t0, t1):
+            nc.vector.quantize_mx(
+                out=words[a][:, t0:t1].bitcast(FP8X4),
+                scales=bytes_all[4 * a : P, t0:t1],
+                in_=rows[a, t0][:].rearrange("p t j -> p (t j)"),
+            )
+
+        def offsets(s0, s1):
+            return offs_sb[:, s0 // 16 : s1 // 16]
+
+        def gather_words(a, s0, s1):
+            nc.vector.tensor_copy(out=slot_words[a][:, s0:s1], in_=words[a][:].indirect(offsets(s0, s1)))
+
+        def gather_bytes(s0, s1):
+            nc.vector.tensor_copy(out=slot_bytes[:, s0:s1], in_=bytes_all[:].indirect(offsets(s0, s1)))
+            for a in (1, 2):
+                nc.sync.dma_start(
+                    out=shifted[a - 1][0 : P - 4 * a, s0:s1].bitcast(I32),
+                    in_=slot_bytes[4 * a : P, s0:s1].bitcast(I32),
+                )
+
+        for t0, t1, engine in parts[0]:
+            cast(0, t0, t1, engine)
+        for t0, t1, engine in parts[0]:
+            quant(0, t0, t1)
+
+        for c in range(len(chunks[2])):
+            load_x(2, c)
         ws_rows = w_scales.rearrange("e a q n -> q (e a) n")
         for q in range(4):
             nc.sync.dma_start(
@@ -87,103 +133,119 @@ def tile_moe_tk_lin_bias_kernel(
         for r in range(TOP):
             nc.sync.dma_start(out=gate_sb[:, r, :], in_=gate_rows[:, r, :])
 
-        def cast(a, c, engine):
-            src = raw[a, c][:].rearrange("p j t -> p t j")
-            if engine == "v":
-                nc.vector.tensor_copy(out=rows[a, c][:], in_=src)
-            else:
-                nc.scalar.copy(out=rows[a, c][:], in_=src)
-
-        def quant(a, c):
-            t0 = sum(chunks[a][:c])
-            width = chunks[a][c]
-            nc.vector.quantize_mx(
-                out=words[a][:, t0 : t0 + width].bitcast(FP8X4),
-                scales=bytes_all[4 * a : P, t0 : t0 + width],
-                in_=rows[a, c][:].rearrange("p t j -> p (t j)"),
-            )
-
-        groups = [(0, 3), (3, 6), (6, 9), (9, 12), (12, 15), (15, 16)]
-
-        def offsets(e0, e1):
-            return offs_sb[:, e0 * C // 16 : e1 * C // 16]
-
-        def gather_words(a, e0, e1):
-            nc.vector.tensor_copy(
-                out=slot_words[a][:, e0 * C : e1 * C], in_=words[a][:].indirect(offsets(e0, e1))
-            )
-
-        cast(0, 0, "v")
-        for c in range(1, 4):
-            cast(0, c, "v")
-            quant(0, c - 1)
-        quant(0, 3)
         for a in (1, 2):
-            for c in range(2):
-                cast(a, c, "s")
-        for e0, e1 in groups:
-            gather_words(0, e0, e1)
-        for a in (1, 2):
-            for c in range(2):
-                quant(a, c)
-        for e0, e1 in groups:
-            cols = slice(e0 * C, e1 * C)
-            nc.vector.tensor_copy(out=slot_bytes[:, cols], in_=bytes_all[:].indirect(offsets(e0, e1)))
-            for a in (1, 2):
-                nc.sync.dma_start(
-                    out=shifted[a - 1][0 : P - 4 * a, cols].bitcast(I32),
-                    in_=slot_bytes[4 * a : P, cols].bitcast(I32),
+            for t0, t1, engine in parts[a]:
+                cast(a, t0, t1, engine)
+        for s0, s1 in ((0, 1536), (1536, 3072), (3072, 4096)):
+            gather_words(0, s0, s1)
+        for t0, t1, engine in parts[1]:
+            quant(1, t0, t1)
+        for s0, s1 in ((0, 1536),):
+            gather_words(1, s0, s1)
+        for t0, t1, engine in parts[2]:
+            quant(2, t0, t1)
+        for s0, s1 in ((0, 1536), (1536, 3072), (3072, 4096)):
+            gather_bytes(s0, s1)
+
+        def multiply(e, h, bank, passes):
+            at = h * 128
+            cols = slice(e * C + at, e * C + at + 128)
+            for a in passes:
+                nc.tensor.matmul_mx(
+                    out=bank,
+                    lhsT=w_sb[:, e * PASSES + a, :].bitcast(FP4X4),
+                    lhsT_scale=ws_sb[:, e * PASSES + a, :],
+                    rhs=slot_words[a][:, cols].bitcast(FP8X4),
+                    rhs_scale=planes[a][:, cols],
+                    start=(a == 0),
+                    stop=(a == PASSES - 1),
                 )
-        for e0, e1 in groups:
-            gather_words(1, e0, e1)
-            gather_words(2, e0, e1)
-            for e in range(e0, e1):
+
+        def expert(e):
+            bank = psum.tile([N, 512], F32, name="bank")
+            for h in range(2):
+                multiply(e, h, bank[:, h * 128 : h * 128 + 128], (0, 1, 2))
+            nc.scalar.activation(
+                out=y[:, e * C : (e + 1) * C], in_=bank[:, 0:C], func=IDENTITY, bias=b_sb[:, e : e + 1]
+            )
+
+        plan = [
+            (2, 0, 768), (2, 768, 1536),
+            (1, 1536, 2304), (2, 1536, 2304),
+            (1, 2304, 3072), (2, 2304, 3072),
+            (1, 3072, 3584), (2, 3072, 3584),
+        ]
+        for a, s0, s1 in plan:
+            gather_words(a, s0, s1)
+            if a == 2:
+                for e in range(s0 // C, s1 // C):
+                    expert(e)
+        gather_words(1, 14 * C, 16 * C)
+        last = {}
+        for e in (14, 15):
+            for h in range(2):
                 bank = psum.tile([N, 512], F32, name="bank")
-                for h in range(2):
-                    cols = slice(e * C + h * 128, e * C + h * 128 + 128)
-                    for a in range(PASSES):
-                        nc.tensor.matmul_mx(
-                            out=bank[:, h * 128 : h * 128 + 128],
-                            lhsT=w_sb[:, e * PASSES + a, :].bitcast(FP4X4),
-                            lhsT_scale=ws_sb[:, e * PASSES + a, :],
-                            rhs=slot_words[a][:, cols].bitcast(FP8X4),
-                            rhs_scale=planes[a][:, cols],
-                            start=(a == 0),
-                            stop=(a == PASSES - 1),
-                        )
-                nc.scalar.activation(
-                    out=y[:, e * C : (e + 1) * C], in_=bank[:, 0:C], func=IDENTITY, bias=b_sb[:, e : e + 1]
+                multiply(e, h, bank[:, 0:128], (0, 1))
+                last[e, h] = bank
+        gather_words(2, 14 * C, 15 * C)
+        for e in (14, 15):
+            for h in range(2):
+                s0 = e * C + h * 128
+                if e == 15:
+                    gather_words(2, s0, s0 + 128)
+                multiply(e, h, last[e, h][:, 0:128], (2,))
+                if (e, h) != (15, 1):
+                    nc.scalar.activation(
+                        out=y[:, s0 : s0 + 128], in_=last[e, h][:, 0:128], func=IDENTITY, bias=b_sb[:, e : e + 1]
+                    )
+                else:
+                    nc.vector.tensor_scalar_add(y[:, s0 : s0 + 128], last[e, h][:, 0:128], b_sb[:, 15:16])
+
+        accs, backs = {}, {}
+
+        def pick(t0, t1, r):
+            prod = keep.tile([P, t1 - t0], F32, name=f"prod{t0}_{r}")
+            nc.vector.tensor_tensor(
+                prod[:], y[:].indirect(pos_sb[r][:, t0 // 16 : t1 // 16]), gate_sb[:, r, t0:t1], MULT
+            )
+            return prod
+
+        def turn_and_add(t0, t1, r, prod, count):
+            for k in range((t1 - t0) // 128):
+                if r == 0:
+                    accs[t0, k] = psum.tile([P, 512], F32, name="bank")
+                nc.tensor.matmul(
+                    accs[t0, k][:, 0:128],
+                    prod[:, k * 128 : k * 128 + 128],
+                    ident[:],
+                    start=(r == 0),
+                    stop=(r == count - 1),
+                    is_transpose=True,
                 )
 
-        halves = [(0, 512), (512, 1024)]
-        prod = {}
-        for i, (t0, t1) in enumerate(halves):
+        def turn_back(t0, t1):
+            turned = keep.tile([P, t1 - t0], F32, name=f"turned{t0}")
+            back = psum.tile([P, 512], F32, name="bank")
+            for k in range((t1 - t0) // 128):
+                sl = slice(k * 128, k * 128 + 128)
+                nc.scalar.copy(turned[:, sl], accs[t0, k][:, 0:128])
+                nc.tensor.transpose(back[:, sl], turned[:, sl], ident[:])
+            return back
+
+        first, second, third = (0, 384), (384, 640), (640, 1024)
+        t0, t1 = third
+        for r in range(3):
+            turn_and_add(t0, t1, r, pick(t0, t1, r), 3)
+        third_back = turn_back(t0, t1)
+        for t0, t1 in (first, second):
             for r in range(TOP):
-                prod[i, r] = keep.tile([P, t1 - t0], F32, name=f"prod{i}_{r}")
-        sums = {}
-        for i, (t0, t1) in enumerate(halves):
-            for s in range(3):
-                sums[i, s] = keep.tile([P, t1 - t0], F32, name=f"sums{i}_{s}")
-
-        def pick(i, r):
-            t0, t1 = halves[i]
-            nc.vector.tensor_tensor(
-                prod[i, r][:], y[:].indirect(pos_sb[r][:, t0 // 16 : t1 // 16]), gate_sb[:, r, t0:t1], MULT
-            )
-
-        def add(i, s):
-            pairs = [(prod[i, 0], prod[i, 1]), (prod[i, 2], prod[i, 3]), (sums[i, 0], sums[i, 1])]
-            nc.vector.tensor_tensor(sums[i, s][:], pairs[s][0][:], pairs[s][1][:], ADD)
-
-        for r in range(TOP):
-            pick(0, r)
-        for r in range(TOP):
-            pick(1, r)
-            if r < 3:
-                add(0, r)
-        t0, t1 = halves[0]
-        nc.sync.dma_start(out=out[:, t0:t1], in_=sums[0, 2][:])
-        for s in range(3):
-            add(1, s)
-        t0, t1 = halves[1]
-        nc.sync.dma_start(out=out[:, t0:t1], in_=sums[1, 2][:])
+                turn_and_add(t0, t1, r, pick(t0, t1, r), TOP)
+            back = turn_back(t0, t1)
+            total = keep.tile([P, t1 - t0], F32, name=f"total{t0}")
+            nc.scalar.copy(total[:], back[:, 0 : t1 - t0])
+            nc.sync.dma_start(out=out[:, t0:t1], in_=total[:])
+        t0, t1 = third
+        prod = pick(t0, t1, 3)
+        total = keep.tile([P, t1 - t0], F32, name=f"total{t0}")
+        nc.vector.tensor_tensor(total[:], third_back[:, 0 : t1 - t0], prod[:], ADD)
+        nc.sync.dma_start(out=out[:, t0:t1], in_=total[:])

@@ -82,12 +82,12 @@ def tile_moe_tk_lin_bias_kernel(
             start = 0
             for c, width in enumerate(chunks[a]):
                 if start <= t0 < start + width:
-                    src = raw[a, c][:, :, t0 - start : t1 - start].rearrange("p j t -> p t j")
+                    src = raw[a, c][:, :, t0 - start : t1 - start].rearrange("p j (c i) -> p c j i", i=4)
                 start += width
             if engine == "v":
-                nc.vector.tensor_copy(out=rows[a, t0][:], in_=src)
+                nc.vector.tensor_copy(out=rows[a, t0][:].rearrange("p (c i) j -> p c j i", i=4), in_=src)
             else:
-                nc.scalar.copy(out=rows[a, t0][:], in_=src)
+                nc.scalar.copy(out=rows[a, t0][:].rearrange("p (c i) j -> p c j i", i=4), in_=src)
 
         def quant(a, t0, t1):
             nc.vector.quantize_mx(
@@ -105,10 +105,11 @@ def tile_moe_tk_lin_bias_kernel(
         def gather_bytes(s0, s1):
             nc.vector.tensor_copy(out=slot_bytes[:, s0:s1], in_=bytes_all[:].indirect(offsets(s0, s1)))
             for a in (1, 2):
-                nc.sync.dma_start(
-                    out=shifted[a - 1][0 : P - 4 * a, s0:s1].bitcast(I32),
-                    in_=slot_bytes[4 * a : P, s0:s1].bitcast(I32),
-                )
+                for q in range(0, P, 32):
+                    nc.sync.dma_start(
+                        out=shifted[a - 1][q : q + 4, s0:s1].bitcast(I32),
+                        in_=slot_bytes[q + 4 * a : q + 4 * a + 4, s0:s1].bitcast(I32),
+                    )
 
         for t0, t1, engine in parts[0]:
             cast(0, t0, t1, engine)
@@ -144,8 +145,6 @@ def tile_moe_tk_lin_bias_kernel(
             gather_words(1, s0, s1)
         for t0, t1, engine in parts[2]:
             quant(2, t0, t1)
-        for s0, s1 in ((0, 1536), (1536, 3072), (3072, 4096)):
-            gather_bytes(s0, s1)
 
         def multiply(e, h, bank, passes):
             at = h * 128
@@ -170,17 +169,21 @@ def tile_moe_tk_lin_bias_kernel(
             )
 
         plan = [
-            (2, 0, 768), (2, 768, 1536),
-            (1, 1536, 2304), (2, 1536, 2304),
+            ("b", 0, 1536), (2, 0, 768),
+            ("b", 1536, 3072), (2, 768, 1536),
+            ("b", 3072, 4096), (1, 1536, 2304), (2, 1536, 2304),
             (1, 2304, 3072), (2, 2304, 3072),
             (1, 3072, 3584), (2, 3072, 3584),
+            (1, 3584, 4096),
         ]
         for a, s0, s1 in plan:
-            gather_words(a, s0, s1)
+            if a == "b":
+                gather_bytes(s0, s1)
+            else:
+                gather_words(a, s0, s1)
             if a == 2:
                 for e in range(s0 // C, s1 // C):
                     expert(e)
-        gather_words(1, 14 * C, 16 * C)
         last = {}
         for e in (14, 15):
             for h in range(2):
@@ -201,10 +204,10 @@ def tile_moe_tk_lin_bias_kernel(
                 else:
                     nc.vector.tensor_scalar_add(y[:, s0 : s0 + 128], last[e, h][:, 0:128], b_sb[:, 15:16])
 
-        accs, backs = {}, {}
+        accs = {}
 
         def pick(t0, t1, r):
-            prod = keep.tile([P, t1 - t0], F32, name=f"prod{t0}_{r}")
+            prod = keep.tile([P, t1 - t0], F32, name=f"prod{t0}_{t1}_{r}")
             nc.vector.tensor_tensor(
                 prod[:], y[:].indirect(pos_sb[r][:, t0 // 16 : t1 // 16]), gate_sb[:, r, t0:t1], MULT
             )
@@ -225,27 +228,31 @@ def tile_moe_tk_lin_bias_kernel(
 
         def turn_back(t0, t1):
             turned = keep.tile([P, t1 - t0], F32, name=f"turned{t0}")
-            back = psum.tile([P, 512], F32, name="bank")
+            backs = []
             for k in range((t1 - t0) // 128):
+                if k % 3 == 0:
+                    back = psum.tile([P, 512], F32, name="bank")
+                    backs.append(back)
                 sl = slice(k * 128, k * 128 + 128)
                 nc.scalar.copy(turned[:, sl], accs[t0, k][:, 0:128])
-                nc.tensor.transpose(back[:, sl], turned[:, sl], ident[:])
-            return back
+                nc.tensor.transpose(backs[-1][:, (k % 3) * 128 : (k % 3) * 128 + 128], turned[:, sl], ident[:])
+            return backs
 
-        first, second, third = (0, 384), (384, 640), (640, 1024)
+        first, third = (0, 384), (384, 1024)
         t0, t1 = third
         for r in range(3):
             turn_and_add(t0, t1, r, pick(t0, t1, r), 3)
-        third_back = turn_back(t0, t1)
-        for t0, t1 in (first, second):
+        third_backs = turn_back(t0, t1)
+        for t0, t1 in (first,):
             for r in range(TOP):
                 turn_and_add(t0, t1, r, pick(t0, t1, r), TOP)
-            back = turn_back(t0, t1)
+            back = turn_back(t0, t1)[0]
             total = keep.tile([P, t1 - t0], F32, name=f"total{t0}")
             nc.scalar.copy(total[:], back[:, 0 : t1 - t0])
             nc.sync.dma_start(out=out[:, t0:t1], in_=total[:])
-        t0, t1 = third
-        prod = pick(t0, t1, 3)
-        total = keep.tile([P, t1 - t0], F32, name=f"total{t0}")
-        nc.vector.tensor_tensor(total[:], third_back[:, 0 : t1 - t0], prod[:], ADD)
-        nc.sync.dma_start(out=out[:, t0:t1], in_=total[:])
+        halves = [(384, 768), (768, 1024)]
+        prods = [pick(t0, t1, 3) for t0, t1 in halves]
+        for (t0, t1), prod, back in zip(halves, prods, third_backs):
+            total = keep.tile([P, t1 - t0], F32, name=f"total{t0}")
+            nc.vector.tensor_tensor(total[:], back[:, 0 : t1 - t0], prod[:], ADD)
+            nc.sync.dma_start(out=out[:, t0:t1], in_=total[:])

@@ -37,7 +37,7 @@ def tile_moe_tk_lin_bias_kernel(
         windows = (2 * T, 2 * T, T)
         words = [keep.tile([P, windows[a]], U32, name=f"words{a}", align_bytes=64) for a in range(PASSES)]
         bytes_all = keep.tile([P, 2 * T], U8, name="bytes_all", align_bytes=64)
-        slot_words = [keep.tile([P, SLOTS], U32, name=f"slot_words{a}", align_bytes=64) for a in range(PASSES)]
+        slot_words = {a: [(0, keep.tile([P, n], U32, name=f"slot_words{a}", align_bytes=64))] for a, n in enumerate((SLOTS, 2048, SLOTS))}
         slot_bytes = keep.tile([P, SLOTS], U8, name="slot_bytes", align_bytes=64)
         shifted = [keep.tile([P, SLOTS], U8, name=f"shifted{a}", align_bytes=64) for a in (1, 2)]
         planes = [slot_bytes, shifted[0], shifted[1]]
@@ -49,11 +49,9 @@ def tile_moe_tk_lin_bias_kernel(
         ident = keep.tile([P, P], F32, name="ident")
 
         nc.vector.memset(words[0][:, T : 2 * T].bitcast(I32), 0)
-        nc.gpsimd.memset(bytes_all[:].bitcast(I32), 0)
+        nc.vector.memset(bytes_all[:].bitcast(I32), 0)
         nc.vector.memset(ws_sb[:].rearrange("p a n -> p (a n)").bitcast(I32), 0)
         nc.vector.memset(words[1][:, T : 2 * T].bitcast(I32), 0)
-        for s in shifted:
-            nc.gpsimd.memset(s[:].bitcast(I32), 0)
         make_identity(nc, ident[:])
 
         chunks = [[512, 256, 256], [512, 512], [512, 512]]
@@ -99,16 +97,20 @@ def tile_moe_tk_lin_bias_kernel(
         def offsets(s0, s1):
             return offs_sb[:, s0 // 16 : s1 // 16]
 
+        def slots_of(a, s0, s1):
+            start, tile = [(start, tile) for start, tile in slot_words[a] if start <= s0][-1]
+            return tile[:, s0 - start : s1 - start]
+
         def gather_words(a, s0, s1):
-            nc.vector.tensor_copy(out=slot_words[a][:, s0:s1], in_=words[a][:].indirect(offsets(s0, s1)))
+            nc.vector.tensor_copy(out=slots_of(a, s0, s1), in_=words[a][:].indirect(offsets(s0, s1)))
 
         def gather_bytes(s0, s1):
             nc.vector.tensor_copy(out=slot_bytes[:, s0:s1], in_=bytes_all[:].indirect(offsets(s0, s1)))
             for a in (1, 2):
-                for q in range(0, P, 32):
+                for p0, p1, move in ((0, 64, 4 * a), (64, 96, 4 * a), (96, 112, 4 * a), (112, 128, 0)):
                     nc.sync.dma_start(
-                        out=shifted[a - 1][q : q + 4, s0:s1].bitcast(I32),
-                        in_=slot_bytes[q + 4 * a : q + 4 * a + 4, s0:s1].bitcast(I32),
+                        out=shifted[a - 1][p0:p1, s0:s1].bitcast(I32),
+                        in_=slot_bytes[p0 + move : p1 + move, s0:s1].bitcast(I32),
                     )
 
         for t0, t1, engine in parts[0]:
@@ -141,10 +143,14 @@ def tile_moe_tk_lin_bias_kernel(
             gather_words(0, s0, s1)
         for t0, t1, engine in parts[1]:
             quant(1, t0, t1)
-        for s0, s1 in ((0, 1536),):
+        for s0, s1 in ((0, 1536), (1536, 2048)):
             gather_words(1, s0, s1)
         for t0, t1, engine in parts[2]:
             quant(2, t0, t1)
+
+        for t0, t1, engine in parts[2]:
+            late = keep.tile([P, 1024], U32, name=f"rows2_{t0}", align_bytes=64)
+            slot_words[1].append((2048 + 2 * t0, late))
 
         def multiply(e, h, bank, passes):
             at = h * 128
@@ -154,7 +160,7 @@ def tile_moe_tk_lin_bias_kernel(
                     out=bank,
                     lhsT=w_sb[:, e * PASSES + a, :].bitcast(FP4X4),
                     lhsT_scale=ws_sb[:, e * PASSES + a, :],
-                    rhs=slot_words[a][:, cols].bitcast(FP8X4),
+                    rhs=slots_of(a, cols.start, cols.stop).bitcast(FP8X4),
                     rhs_scale=planes[a][:, cols],
                     start=(a == 0),
                     stop=(a == PASSES - 1),
@@ -169,12 +175,10 @@ def tile_moe_tk_lin_bias_kernel(
             )
 
         plan = [
-            ("b", 0, 1536), (2, 0, 768),
-            ("b", 1536, 3072), (2, 768, 1536),
-            ("b", 3072, 4096), (1, 1536, 2304), (2, 1536, 2304),
-            (1, 2304, 3072), (2, 2304, 3072),
-            (1, 3072, 3584), (2, 3072, 3584),
-            (1, 3584, 4096),
+            ("b", 0, 1536), ("b", 1536, 3072), (2, 0, 768),
+            ("b", 3072, 4096), (2, 768, 1536), (2, 1536, 2048),
+            (1, 2048, 3072), (2, 2048, 2560), (2, 2560, 3072),
+            (1, 3072, 4096),
         ]
         for a, s0, s1 in plan:
             if a == "b":
@@ -190,6 +194,9 @@ def tile_moe_tk_lin_bias_kernel(
                 bank = psum.tile([N, 512], F32, name="bank")
                 multiply(e, h, bank[:, 0:128], (0, 1))
                 last[e, h] = bank
+        gather_words(2, 12 * C, 14 * C)
+        for e in (12, 13):
+            expert(e)
         gather_words(2, 14 * C, 15 * C)
         for e in (14, 15):
             for h in range(2):

@@ -233,33 +233,36 @@ def tile_moe_tk_lin_bias_kernel(
                     is_transpose=True,
                 )
 
-        def turn_back(t0, t1):
+        def turn_back(t0, t1, per_bank=4):
             turned = keep.tile([P, t1 - t0], F32, name=f"turned{t0}")
             backs = []
             for k in range((t1 - t0) // 128):
-                if k % 3 == 0:
+                m = k % per_bank
+                if m == 0:
                     back = psum.tile([P, 512], F32, name="bank")
-                    backs.append(back)
+                    backs.append((back, 128 * min(per_bank, (t1 - t0) // 128 - k)))
                 sl = slice(k * 128, k * 128 + 128)
                 nc.scalar.copy(turned[:, sl], accs[t0, k][:, 0:128])
-                nc.tensor.transpose(backs[-1][:, (k % 3) * 128 : (k % 3) * 128 + 128], turned[:, sl], ident[:])
+                nc.tensor.transpose(back[:, m * 128 : m * 128 + 128], turned[:, sl], ident[:])
             return backs
 
-        first, third = (0, 384), (384, 1024)
+        first, third = (0, 512), (512, 1024)
+        t0, t1 = first
+        for r in range(TOP):
+            turn_and_add(t0, t1, r, pick(t0, t1, r), TOP)
+        total = keep.tile([P, t1 - t0], F32, name=f"total{t0}")
+        at = 0
+        for back, width in turn_back(t0, t1):
+            nc.scalar.copy(total[:, at : at + width], back[:, 0:width])
+            at += width
+        nc.sync.dma_start(out=out[:, t0:t1], in_=total[:])
         t0, t1 = third
         for r in range(3):
             turn_and_add(t0, t1, r, pick(t0, t1, r), 3)
-        third_backs = turn_back(t0, t1)
-        for t0, t1 in (first,):
-            for r in range(TOP):
-                turn_and_add(t0, t1, r, pick(t0, t1, r), TOP)
-            back = turn_back(t0, t1)[0]
-            total = keep.tile([P, t1 - t0], F32, name=f"total{t0}")
-            nc.scalar.copy(total[:], back[:, 0 : t1 - t0])
-            nc.sync.dma_start(out=out[:, t0:t1], in_=total[:])
-        halves = [(384, 768), (768, 1024)]
+        third_backs = turn_back(t0, t1, 2)
+        halves = [(512, 768), (768, 1024)]
         prods = [pick(t0, t1, 3) for t0, t1 in halves]
-        for (t0, t1), prod, back in zip(halves, prods, third_backs):
+        for (t0, t1), prod, (back, width) in zip(halves, prods, third_backs):
             total = keep.tile([P, t1 - t0], F32, name=f"total{t0}")
-            nc.vector.tensor_tensor(total[:], back[:, 0 : t1 - t0], prod[:], ADD)
+            nc.vector.tensor_tensor(total[:], back[:, 0:width], prod[:], ADD)
             nc.sync.dma_start(out=out[:, t0:t1], in_=total[:])

from contextlib import ExitStack

import concourse.mybir as mybir
from concourse.masks import make_identity

K, T, E, C, N, TOP = 1536, 1024, 16, 256, 128, 4
SLOTS = E * C
P = 128
PASSES = 3
K_PASS = 512
FLOPS = 2 * SLOTS * K * N

F32 = mybir.dt.float32
BF16 = mybir.dt.bfloat16
U32 = mybir.dt.uint32
I32 = mybir.dt.int32
U16 = mybir.dt.uint16
U8 = mybir.dt.uint8
FP8X4 = mybir.dt.float8_e4m3fn_x4
FP4X4 = mybir.dt.float4_e2m1fn_x4
MULT = mybir.AluOpType.mult
ADD = mybir.AluOpType.add
IDENTITY = mybir.ActivationFunctionType.Identity


def tile_moe_tk_lin_bias_kernel(
    tc, xT, w_words, w_scales, b, gate, offs, pos1, pos2, pos3, pos4, out
):
    nc = tc.nc
    with ExitStack() as ctx:
        keep = ctx.enter_context(tc.tile_pool(name="keep", bufs=1))
        stage = ctx.enter_context(tc.tile_pool(name="stage", bufs=4))
        psum = ctx.enter_context(tc.psum_pool(name="psum", bufs=8))

        offs_sb = keep.tile([P, SLOTS // 16], U16, name="offs_sb")
        pos_sb = [keep.tile([P, T // 16], U16, name=f"pos_sb{r}") for r in range(TOP)]
        windows = (2 * T, 2 * T, T)
        words = [keep.tile([P, windows[a]], U32, name=f"words{a}", align_bytes=64) for a in range(PASSES)]
        bytes_all = keep.tile([P, 2 * T], U8, name="bytes_all", align_bytes=64)
        slot_words = {a: [(0, keep.tile([P, n], U32, name=f"slot_words{a}", align_bytes=64))] for a, n in enumerate((SLOTS, 2048, SLOTS))}
        slot_bytes = keep.tile([P, SLOTS], U8, name="slot_bytes", align_bytes=64)
        shifted = [keep.tile([P, SLOTS], U8, name=f"shifted{a}", align_bytes=64) for a in (1, 2)]
        planes = [slot_bytes, shifted[0], shifted[1]]
        w_sb = keep.tile([P, E * PASSES, 2 * N], U8, name="w_sb", align_bytes=64)
        ws_sb = keep.tile([P, E * PASSES, N], U8, name="ws_sb", align_bytes=64)
        b_sb = keep.tile([P, E], F32, name="b_sb")
        gate_sb = keep.tile([P, TOP, T], F32, name="gate_sb")
        y = keep.tile([P, SLOTS], F32, name="y")
        ident = keep.tile([P, P], F32, name="ident")

        nc.vector.memset(words[0][:, T : 2 * T].bitcast(I32), 0)
        nc.vector.memset(bytes_all[:].bitcast(I32), 0)
        nc.vector.memset(ws_sb[:].rearrange("p a n -> p (a n)").bitcast(I32), 0)
        nc.vector.memset(words[1][:, T : 2 * T].bitcast(I32), 0)
        make_identity(nc, ident[:])

        chunks = [[512, 256, 256], [512, 512], [512, 512]]
        parts = [
            [(0, 256, "v"), (256, 512, "s"), (512, 768, "v"), (768, 896, "v"), (896, 1024, "s")],
            [(0, 512, "s"), (512, 1024, "s")],
            [(0, 512, "s"), (512, 1024, "s")],
        ]
        raw, rows = {}, {}

        def load_x(a, c):
            t0 = sum(chunks[a][:c])
            width = chunks[a][c]
            raw[a, c] = stage.tile([P, 4, width], F32, name=f"raw{width}")
            view = xT[a * K_PASS : (a + 1) * K_PASS, t0 : t0 + width]
            nc.sync.dma_start(out=raw[a, c][:], in_=view.rearrange("(p j) t -> p j t", j=4))

        for c in range(len(chunks[0])):
            load_x(0, c)
        nc.sync.dma_start(offs_sb[:], offs)
        for c in range(len(chunks[1])):
            load_x(1, c)

        def cast(a, t0, t1, engine):
            rows[a, t0] = keep.tile([P, t1 - t0, 4], BF16, name=f"rows{a}_{t0}", align_bytes=64)
            start = 0
            for c, width in enumerate(chunks[a]):
                if start <= t0 < start + width:
                    src = raw[a, c][:, :, t0 - start : t1 - start].rearrange("p j (c i) -> p c j i", i=4)
                start += width
            if engine == "v":
                nc.vector.tensor_copy(out=rows[a, t0][:].rearrange("p (c i) j -> p c j i", i=4), in_=src)
            else:
                nc.scalar.copy(out=rows[a, t0][:].rearrange("p (c i) j -> p c j i", i=4), in_=src)

        def quant(a, t0, t1):
            nc.vector.quantize_mx(
                out=words[a][:, t0:t1].bitcast(FP8X4),
                scales=bytes_all[4 * a : P, t0:t1],
                in_=rows[a, t0][:].rearrange("p t j -> p (t j)"),
            )

        def offsets(s0, s1):
            return offs_sb[:, s0 // 16 : s1 // 16]

        def slots_of(a, s0, s1):
            start, tile = [(start, tile) for start, tile in slot_words[a] if start <= s0][-1]
            return tile[:, s0 - start : s1 - start]

        def gather_words(a, s0, s1):
            nc.vector.tensor_copy(out=slots_of(a, s0, s1), in_=words[a][:].indirect(offsets(s0, s1)))

        def gather_bytes(s0, s1):
            nc.vector.tensor_copy(out=slot_bytes[:, s0:s1], in_=bytes_all[:].indirect(offsets(s0, s1)))
            for a in (1, 2):
                for p0, p1, move in ((0, 64, 4 * a), (64, 96, 4 * a), (96, 112, 4 * a), (112, 128, 0)):
                    nc.sync.dma_start(
                        out=shifted[a - 1][p0:p1, s0:s1].bitcast(I32),
                        in_=slot_bytes[p0 + move : p1 + move, s0:s1].bitcast(I32),
                    )

        for t0, t1, engine in parts[0]:
            cast(0, t0, t1, engine)
        for t0, t1, engine in parts[0]:
            quant(0, t0, t1)

        for c in range(len(chunks[2])):
            load_x(2, c)
        ws_rows = w_scales.rearrange("e a q n -> q (e a) n")
        for q in range(4):
            nc.sync.dma_start(
                out=ws_sb[32 * q : 32 * q + 4, :, :].bitcast(I32), in_=ws_rows[4 * q : 4 * q + 4].bitcast(I32)
            )
        w_rows = w_words.rearrange("e a p c -> p (e a) c")
        for g in range(4):
            sl = slice(12 * g, 12 * g + 12)
            nc.sync.dma_start(out=w_sb[:, sl, :].bitcast(I32), in_=w_rows[:, sl, :].bitcast(I32))
        nc.sync.dma_start(b_sb[:], b)
        for r, p in enumerate((pos1, pos2, pos3, pos4)):
            nc.sync.dma_start(pos_sb[r][:], p)
        gate_rows = gate.rearrange("r p t -> p r t")
        for r in range(TOP):
            nc.sync.dma_start(out=gate_sb[:, r, :], in_=gate_rows[:, r, :])

        for a in (1, 2):
            for t0, t1, engine in parts[a]:
                cast(a, t0, t1, engine)
        for s0, s1 in ((0, 1536), (1536, 3072), (3072, 4096)):
            gather_words(0, s0, s1)
        for t0, t1, engine in parts[1]:
            quant(1, t0, t1)
        for s0, s1 in ((0, 1536), (1536, 2048)):
            gather_words(1, s0, s1)
        for t0, t1, engine in parts[2]:
            quant(2, t0, t1)

        for t0, t1, engine in parts[2]:
            late = keep.tile([P, 1024], U32, name=f"rows2_{t0}", align_bytes=64)
            slot_words[1].append((2048 + 2 * t0, late))

        def multiply(e, h, bank, passes):
            at = h * 128
            cols = slice(e * C + at, e * C + at + 128)
            for a in passes:
                nc.tensor.matmul_mx(
                    out=bank,
                    lhsT=w_sb[:, e * PASSES + a, :].bitcast(FP4X4),
                    lhsT_scale=ws_sb[:, e * PASSES + a, :],
                    rhs=slots_of(a, cols.start, cols.stop).bitcast(FP8X4),
                    rhs_scale=planes[a][:, cols],
                    start=(a == 0),
                    stop=(a == PASSES - 1),
                )

        def expert(e):
            bank = psum.tile([N, 512], F32, name="bank")
            for h in range(2):
                multiply(e, h, bank[:, h * 128 : h * 128 + 128], (0, 1, 2))
            nc.scalar.activation(
                out=y[:, e * C : (e + 1) * C], in_=bank[:, 0:C], func=IDENTITY, bias=b_sb[:, e : e + 1]
            )

        plan = [
            ("b", 0, 1536), ("b", 1536, 3072), (2, 0, 768),
            ("b", 3072, 4096), (2, 768, 1536), (2, 1536, 2048),
            (1, 2048, 3072), (2, 2048, 2560), (2, 2560, 3072),
            (1, 3072, 4096),
        ]
        for a, s0, s1 in plan:
            if a == "b":
                gather_bytes(s0, s1)
            else:
                gather_words(a, s0, s1)
            if a == 2:
                for e in range(s0 // C, s1 // C):
                    expert(e)
        last = {}
        for e in (14, 15):
            for h in range(2):
                bank = psum.tile([N, 512], F32, name="bank")
                multiply(e, h, bank[:, 0:128], (0, 1))
                last[e, h] = bank
        gather_words(2, 12 * C, 14 * C)
        for e in (12, 13):
            expert(e)
        gather_words(2, 14 * C, 15 * C)
        for e in (14, 15):
            for h in range(2):
                s0 = e * C + h * 128
                if e == 15:
                    gather_words(2, s0, s0 + 128)
                multiply(e, h, last[e, h][:, 0:128], (2,))
                if (e, h) != (15, 1):
                    nc.scalar.activation(
                        out=y[:, s0 : s0 + 128], in_=last[e, h][:, 0:128], func=IDENTITY, bias=b_sb[:, e : e + 1]
                    )
                else:
                    nc.vector.tensor_scalar_add(y[:, s0 : s0 + 128], last[e, h][:, 0:128], b_sb[:, 15:16])

        accs = {}

        def pick(t0, t1, r):
            prod = keep.tile([P, t1 - t0], F32, name=f"prod{t0}_{t1}_{r}")
            nc.vector.tensor_tensor(
                prod[:], y[:].indirect(pos_sb[r][:, t0 // 16 : t1 // 16]), gate_sb[:, r, t0:t1], MULT
            )
            return prod

        def turn_and_add(t0, t1, r, prod, count):
            for k in range((t1 - t0) // 128):
                if r == 0:
                    accs[t0, k] = psum.tile([P, 512], F32, name="bank")
                nc.tensor.matmul(
                    accs[t0, k][:, 0:128],
                    prod[:, k * 128 : k * 128 + 128],
                    ident[:],
                    start=(r == 0),
                    stop=(r == count - 1),
                    is_transpose=True,
                )

        def turn_back(t0, t1, per_bank=4):
            turned = keep.tile([P, t1 - t0], F32, name=f"turned{t0}")
            backs = []
            for k in range((t1 - t0) // 128):
                m = k % per_bank
                if m == 0:
                    back = psum.tile([P, 512], F32, name="bank")
                    backs.append((back, 128 * min(per_bank, (t1 - t0) // 128 - k)))
                sl = slice(k * 128, k * 128 + 128)
                nc.scalar.copy(turned[:, sl], accs[t0, k][:, 0:128])
                nc.tensor.transpose(back[:, m * 128 : m * 128 + 128], turned[:, sl], ident[:])
            return backs

        first, third = (0, 512), (512, 1024)
        t0, t1 = first
        for r in range(TOP):
            turn_and_add(t0, t1, r, pick(t0, t1, r), TOP)
        total = keep.tile([P, t1 - t0], F32, name=f"total{t0}")
        at = 0
        for back, width in turn_back(t0, t1):
            nc.scalar.copy(total[:, at : at + width], back[:, 0:width])
            at += width
        nc.sync.dma_start(out=out[:, t0:t1], in_=total[:])
        t0, t1 = third
        for r in range(3):
            turn_and_add(t0, t1, r, pick(t0, t1, r), 3)
        third_backs = turn_back(t0, t1, 2)
        halves = [(512, 768), (768, 1024)]
        prods = [pick(t0, t1, 3) for t0, t1 in halves]
        for (t0, t1), prod, (back, width) in zip(halves, prods, third_backs):
            total = keep.tile([P, t1 - t0], F32, name=f"total{t0}")
            nc.vector.tensor_tensor(total[:], back[:, 0:width], prod[:], ADD)
            nc.sync.dma_start(out=out[:, t0:t1], in_=total[:])
